import numpy as np
import ml_dtypes


def mxq(x, axis, fmt="e4m3"):
    dtype, down = {"e4m3": (ml_dtypes.float8_e4m3fn, 7), "e5m2": (ml_dtypes.float8_e5m2, 14)}[fmt]
    v = np.moveaxis(np.asarray(x, np.float32).astype(ml_dtypes.bfloat16).astype(np.float64), axis, -1)
    blocks = v.reshape(v.shape[:-1] + (-1, 32))
    amax = np.abs(blocks).max(-1, keepdims=True)
    byte = np.maximum(np.where(amax > 0, np.frexp(amax)[1] - 1 + 127, 0) - down, 1)
    scale = np.exp2(byte - 127.0)
    codes = (blocks / scale).astype(np.float32).astype(dtype).astype(np.float64)
    return np.moveaxis((codes * scale).reshape(v.shape), -1, axis)


WIDE = False


def mx_kscale(k):
    if not WIDE:
        return np.ones(k)
    levels = np.array([10, -10, 5, -5, 0])
    if k % 512:
        return np.exp2(np.random.permutation(np.resize(levels, k // 32))).repeat(32)
    a = np.empty((k // 512, 16))
    for p in range(k // 512):
        a[p, :8] = np.random.permutation(np.resize(levels, 8))
        for g in range(8):
            far = levels[np.abs(levels - a[p, g]) >= 10]
            a[p, g + 8] = far[np.random.randint(len(far))]
    return np.exp2(a.ravel()).repeat(32)


BF16 = ml_dtypes.bfloat16


def bf(x):
    return np.asarray(x, np.float32).astype(BF16)


def f64(x):
    return np.asarray(x).astype(np.float64)

def planes(Y):
    n, m = Y.shape
    b = f64(bf(Y)).reshape(n // 32, 32, m)
    amax = np.abs(b).max(1)
    byte = np.clip(np.where(amax > 0, np.frexp(amax)[1] - 1 + 127 - 7, 1), 1, 254)
    codes = (b * np.exp2(127.0 - byte)[:, None, :]).reshape(n, m).astype(np.float32).astype(ml_dtypes.float8_e4m3fn).view(np.uint8)
    words = codes.reshape(n // 512, 128, 4, m).transpose(0, 1, 3, 2)
    return np.ascontiguousarray(words), np.ascontiguousarray(byte.astype(np.uint8).reshape(n // 512, 16, m))


E, K, N = 1024, 1024, 1536


def noise(*shape):
    return np.random.randn(*shape)

def setup_inputs():
    s = mx_kscale(K)
    spread = np.exp(0.8 * noise(N))
    displacement = noise(E, K) / s
    velocity = noise(E, K) / s
    gradient = noise(K, N) / np.sqrt(K) * s[:, None]
    stiffness = spread * np.exp(0.3 * noise(E, N))
    relaxation = 0.6 * np.exp(0.3 * noise(N))
    prestress = 0.4 * spread * noise(N)
    return {
        "displacement": bf(displacement),
        "velocity": bf(velocity),
        "gradient": bf(gradient),
        "stiffness": bf(stiffness),
        "relaxation": bf(relaxation),
        "prestress": bf(prestress),
    }

def reference(displacement, velocity, gradient, stiffness, relaxation, prestress):
    uq = mxq(f64(displacement), 1, "e4m3")
    vq = mxq(f64(velocity), 1, "e4m3")
    gq = mxq(f64(gradient), 0, "e4m3")
    strain = uq @ gq
    rate = vq @ gq
    y = f64(stiffness) * (strain + f64(relaxation) * rate) + f64(prestress)
    Y = y.T
    words, scales = planes(Y)
    return y, words, scales

@@ -1,0 +1,386 @@
+from contextlib import ExitStack
+
+import concourse.mybir as mybir
+from concourse.masks import make_identity
+
+E, K, N = 1024, 1024, 1536
+FLOPS = 2 * 2 * E * K * N
+
+F32 = mybir.dt.float32
+BF16 = mybir.dt.bfloat16
+U32 = mybir.dt.uint32
+I32 = mybir.dt.int32
+U8 = mybir.dt.uint8
+FP8X4 = mybir.dt.float8_e4m3fn_x4
+ALU = mybir.AluOpType
+ACT = mybir.ActivationFunctionType
+
+P = 128
+PACK = 4
+GROUP = P * PACK
+PASSES = K // GROUP
+GROUPS = N // GROUP
+CHUNK = 256
+BANK = 512
+
+X_LAG = 0
+CHUNKS = E // CHUNK
+TILES = CHUNK // P
+PAIRS = sorted([(ch, g) for ch in range(CHUNKS) for g in range(GROUPS)], key=lambda s: (max(2 * s[0], 2 * s[1] + 1), s))
+SPLIT = 0
+G_SCALAR = [(g, c, 1) for g in range(GROUPS) for c in range(PASSES)]
+ADDC = ["GG", "GG"]
+TAIL = ["AA", "VV"]
+WARM = 0
+G_FIRST = 0
+N_WORK = 3
+N_Y = 3
+N_STAGE = 6
+N_OUT = 8
+
+
+def tile_kelvin_voigt_element_stress_g1_kernel(
+    tc, displacement, velocity, gradient, stiffness, relaxation, prestress, out_0, out_1, out_2
+):
+    nc = tc.nc
+    STEPS = [(ch * CHUNK, CHUNK, g) for ch, g in PAIRS[: len(PAIRS) - SPLIT]]
+    STEPS = STEPS + [(ch * CHUNK + j * P, P, g) for ch, g in PAIRS[len(PAIRS) - SPLIT :] for j in range(TILES)]
+    with ExitStack() as ctx:
+        sb = ctx.enter_context(tc.tile_pool(name="sb", bufs=1))
+        ps = ctx.enter_context(tc.psum_pool(name="ps", bufs=1))
+        ctx.enter_context(tc.manual_schedule())
+
+        def sbuf(name, shape, dtype):
+            return sb.tile(shape, dtype, name=name, align_bytes=64)
+
+        def ring(name, count, shape, dtype):
+            return [sbuf("%s%d" % (name, i), shape, dtype) for i in range(count)]
+
+        banks = [ps.tile([P, BANK], F32, name="bank%d" % i) for i in range(8)]
+        rate_banks, strain_banks, d_bank, turn_banks = banks[0:2], banks[2:4], banks[4], banks[5:8]
+        modes = {"v": velocity, "u": displacement}
+
+        x_raw = {(op, j): sbuf("x_raw_%s%d" % (op, j), [P, K], BF16) for op in modes for j in range(E // P)}
+        x_codes = {(op, c): sbuf("x_codes_%s%d" % (op, c), [P, E], U32) for op in modes for c in range(PASSES)}
+        x_scales = {(op, c): sbuf("x_scales_%s%d" % (op, c), [P, E], U8) for op in modes for c in range(PASSES)}
+        gc = [(g, c) for g in range(GROUPS) for c in range(PASSES)]
+        g_raw = {(g, c): sbuf("g_raw%d%d" % (g, c), [P, PACK, GROUP], BF16) for g, c in gc}
+        g_codes = {(g, c): sbuf("g_codes%d%d" % (g, c), [P, GROUP], U32) for g, c in gc}
+        g_scales = {(g, c): sbuf("g_scales%d%d" % (g, c), [P, GROUP], U8) for g, c in gc}
+        d_raw = [sbuf("d_raw%d" % s, [P, w // P, GROUP], BF16) for s, (e0, w, g) in enumerate(STEPS)]
+        rc_raw = {name: sbuf("raw_" + name, [P, GROUPS, PACK], BF16) for name in ("r", "c")}
+        rc = {name: sbuf("col_" + name, [P, GROUPS * PACK], F32) for name in ("r", "c")}
+        ident = sbuf("ident", [P, P], F32)
+        work = ring("work", N_WORK, [P, PACK * CHUNK], F32)
+        y_turned = ring("y_turned", N_Y, [P, PACK * CHUNK], F32)
+        stage = ring("stage", N_STAGE, [P, PACK * CHUNK], BF16)
+        y_out = ring("y_out", N_OUT, [P, GROUP], F32)
+        y_codes = [sbuf("y_codes%d" % s, [P, w], U32) for s, (e0, w, g) in enumerate(STEPS)]
+        y_scales = ring("y_scales", GROUPS, [P, E], U8)
+        count = {"turn": 0, "stage": 0, "out": 0}
+
+        def take(name, tiles):
+            count[name] = count[name] + 1
+            return tiles[(count[name] - 1) % len(tiles)]
+
+        make_identity(nc, ident[:])
+
+        def load_x(op, ch):
+            for j in range(ch * TILES, (ch + 1) * TILES):
+                nc.sync.dma_start(out=x_raw[op, j][:], in_=modes[op][j * P : (j + 1) * P, :])
+
+        def load_g(g, c):
+            rows = gradient[c * GROUP : (c + 1) * GROUP, g * GROUP : (g + 1) * GROUP]
+            nc.sync.dma_start(out=g_raw[g, c][:], in_=rows.rearrange("(p j) n -> p j n", j=PACK))
+
+        def load_d(s):
+            e0, w, g = STEPS[s]
+            rows = stiffness[e0 : e0 + w, g * GROUP : (g + 1) * GROUP]
+            nc.sync.dma_start(out=d_raw[s][:], in_=rows.rearrange("(j p) n -> p j n", p=P))
+
+        first_ch = {ch: min(s for s in range(len(STEPS)) if STEPS[s][0] // CHUNK == ch) for ch in range(CHUNKS)}
+        first_g = {g: min(s for s in range(len(STEPS)) if STEPS[s][2] == g) for g in range(GROUPS)}
+        last_g = {g: max(s for s in range(len(STEPS)) if STEPS[s][2] == g) for g in range(GROUPS)}
+
+        for s, (e0, w, g) in enumerate(STEPS):
+            ch = e0 // CHUNK
+            for c, op in enumerate(modes):
+                if first_ch[ch] == s:
+                    load_x(op, ch)
+                if first_g[g] == s:
+                    load_g(g, c)
+            if s == 0:
+                for name, vec in (("r", relaxation), ("c", prestress)):
+                    nc.sync.dma_start(out=rc_raw[name][:], in_=vec.rearrange("(g p t) -> p g t", p=P, t=PACK))
+            load_d(s)
+
+        def quantize(codes, scales, src):
+            nc.vector.quantize_mx(out=codes.bitcast(FP8X4), scales=scales, in_=src)
+
+        def g_interleave(g, c, u, dst, on_scalar):
+            src = g_raw[g, c][:].rearrange("p j (a b t) -> p a t b j", b=2, t=PACK)[:, :, 2 * u : 2 * u + 2, :, :]
+            out = dst[:].rearrange("p (t a b j) -> p a t b j", t=2, b=2, j=PACK)
+            if on_scalar:
+                nc.scalar.copy(out=out, in_=src)
+            else:
+                nc.vector.tensor_copy(out=out, in_=src)
+
+        def g_quantize(g, c, u, src):
+            cols = slice(2 * u * P, 2 * (u + 1) * P)
+            quantize(g_codes[g, c][:, cols], g_scales[g, c][:, cols], src[:])
+
+        def x_turn(op, c, ch, bank):
+            for i in range(TILES):
+                words = x_raw[op, ch * TILES + i][:].bitcast(F32)
+                for u in range(2):
+                    nc.tensor.transpose(
+                        bank[:, u * CHUNK + i * P : u * CHUNK + (i + 1) * P],
+                        words[:, 256 * c + u : 256 * (c + 1) : 2],
+                        ident[:],
+                    )
+
+        def x_copy(bank, dst):
+            nc.scalar.copy(
+                out=dst[:].bitcast(F32).rearrange("p (e u) -> p e u", u=2),
+                in_=bank[:].rearrange("p (u e) -> p e u", u=2),
+            )
+
+        def x_quantize(op, c, ch, src):
+            cols = slice(ch * CHUNK, (ch + 1) * CHUNK)
+            quantize(x_codes[op, c][:, cols], x_scales[op, c][:, cols], src[:])
+
+        def slot(s, t, n=1):
+            return slice(t * STEPS[s][1], (t + n) * STEPS[s][1])
+
+        def tiles(s):
+            return range(STEPS[s][1] // P)
+
+        def multiply(s, by_pair):
+            e0, w, g = STEPS[s]
+            cols = slice(e0, e0 + w)
+            order = [(op, pair, u) for op, pair in (("v", rate_banks), ("u", strain_banks)) for u in range(2)]
+            if by_pair:
+                order = sorted(order, key=lambda item: item[2])
+            for op, pair, u in order:
+                for t in (2 * u, 2 * u + 1):
+                    for c in range(PASSES):
+                        nc.tensor.matmul_mx(
+                            out=pair[t // 2][:, slot(s, t % 2)],
+                            lhsT=g_codes[g, c][:, t * P : (t + 1) * P].bitcast(FP8X4),
+                            lhsT_scale=g_scales[g, c][:, t * P : (t + 1) * P],
+                            rhs=x_codes[op, c][:, cols].bitcast(FP8X4),
+                            rhs_scale=x_scales[op, c][:, cols],
+                            start=(c == 0),
+                            stop=(c == PASSES - 1),
+                        )
+
+        def col(name, s, t):
+            i = STEPS[s][2] * PACK + t
+            return rc[name][:, i : i + 1]
+
+        def half(s, u):
+            return work[s % N_WORK][:, slot(s, 2 * u, 2)]
+
+        def scale_rate(s, u):
+            for t in (2 * u, 2 * u + 1):
+                nc.scalar.activation(
+                    out=work[s % N_WORK][:, slot(s, t)], in_=rate_banks[u][:, slot(s, t % 2)], func=ACT.Copy, scale=col("r", s, t)
+                )
+
+        def add_strain(s, u):
+            nc.vector.tensor_tensor(out=half(s, u), in0=strain_banks[u][:, slot(s, 0, 2)], in1=half(s, u), op=ALU.add)
+
+        def d_turn(s, bank):
+            w = STEPS[s][1]
+            for j in range(w // P):
+                words = d_raw[s][:, j, :].bitcast(F32)
+                for u in range(2):
+                    nc.tensor.transpose(
+                        bank[:, u * w + j * P : u * w + (j + 1) * P], words[:, u : GROUP // 2 : 2], ident[:]
+                    )
+
+        def times_d(s, u, bank):
+            pairs = bank[:, slot(s, u)].bitcast(BF16).rearrange("p (e i) -> p i e", i=2)
+            acc = half(s, u).rearrange("p (i e) -> p i e", i=2)
+            nc.vector.tensor_tensor(out=acc, in0=pairs, in1=acc, op=ALU.mult)
+
+        def add_c(s, u, engines):
+            for t in (2 * u, 2 * u + 1):
+                src, dst = work[s % N_WORK][:, slot(s, t)], y_turned[s % N_Y][:, slot(s, t)]
+                if engines[t % 2] == "G":
+                    nc.gpsimd.tensor_scalar(out=dst, in0=src, scalar1=1.0, scalar2=col("c", s, t), op0=ALU.mult, op1=ALU.add)
+                elif engines[t % 2] == "V":
+                    nc.vector.tensor_scalar(out=dst, in0=src, scalar1=col("c", s, t), scalar2=None, op0=ALU.add)
+                else:
+                    nc.scalar.activation(out=dst, in_=src, func=ACT.Identity, bias=col("c", s, t))
+
+        def y_turn(s, j, bank, slots):
+            for t in slots:
+                lo = t * STEPS[s][1] + j * P
+                nc.tensor.transpose(bank[:, t * P : (t + 1) * P], y_turned[s % N_Y][:, lo : lo + P], ident[:])
+
+        def y_copy(s, j, bank):
+            e0, w, g = STEPS[s]
+            dst = take("out", y_out)
+            nc.scalar.copy(out=dst[:].rearrange("e (p t) -> e p t", t=PACK), in_=bank[:].rearrange("e (t p) -> e p t", t=PACK))
+            lo = e0 + j * P
+            nc.sync.dma_start(out=out_0[lo : lo + P, g * GROUP : (g + 1) * GROUP], in_=dst[:])
+
+        def y_interleave(s, dst):
+            nc.vector.tensor_copy(
+                out=dst[:, slot(s, 0, PACK)].rearrange("p (a i t) -> p a t i", i=4, t=PACK),
+                in_=y_turned[s % N_Y][:, slot(s, 0, PACK)].rearrange("p (t a i) -> p a t i", t=PACK, i=4),
+            )
+
+        def y_quantize(s, src):
+            e0, w, g = STEPS[s]
+            cols = slice(e0, e0 + w)
+            quantize(y_codes[s][:], y_scales[g][:, cols], src[:, slot(s, 0, PACK)])
+            words = out_1[g, :, cols, :].rearrange("p m t -> p (m t)").bitcast(I32)
+            nc.sync.dma_start(out=words, in_=y_codes[s][:].bitcast(I32))
+            if last_g[g] == s:
+                for q in range(4):
+                    nc.sync.dma_start(
+                        out=out_2[g, 4 * q : 4 * q + 4, :].bitcast(I32),
+                        in_=y_scales[g][32 * q : 32 * q + 4, :].bitcast(I32),
+                    )
+
+        waiting = []
+
+        def quantize_waiting(keep=0):
+            while len(waiting) > keep:
+                waiting.pop(0)()
+
+        def g_piece(g, c, u):
+            dst = take("stage", stage)
+            g_interleave(g, c, u, dst, (g, c, u) in G_SCALAR)
+            waiting.append(lambda: g_quantize(g, c, u, dst))
+
+        def x_out(op, c, ch, bank):
+            dst = take("stage", stage)
+            x_copy(bank, dst)
+            waiting.append(lambda: x_quantize(op, c, ch, dst))
+
+        for i, op in enumerate(modes):
+            for c in range(PASSES):
+                x_turn(op, c, 0, banks[PASSES * i + c])
+            x_out(op, 0, 0, banks[PASSES * i])
+            quantize_waiting(keep=1)
+            g_piece(0, i, 0)
+            x_out(op, 1, 0, banks[PASSES * i + 1])
+            g_piece(0, i, 1)
+        quantize_waiting(keep=1)
+        for name in ("r", "c"):
+            nc.vector.tensor_copy(out=rc[name][:], in_=rc_raw[name][:].rearrange("p g t -> p (g t)"))
+        quantize_waiting()
+        for i in range(WARM):
+            nc.tensor.matmul_mx(
+                out=turn_banks[0][:, 0:CHUNK],
+                lhsT=g_codes[0, 0][:, 0:P].bitcast(FP8X4),
+                lhsT_scale=g_scales[0, 0][:, 0:P],
+                rhs=x_codes["v", 0][:, 0:CHUNK].bitcast(FP8X4),
+                rhs_scale=x_scales["v", 0][:, 0:CHUNK],
+                start=True,
+                stop=True,
+            )
+        last = len(STEPS) - 1
+        d_banks = {s: d_bank for s in range(last)}
+        d_banks[last] = turn_banks[2]
+        d_turn(0, d_banks[0])
+
+        x_todo = [(op, c, ch) for ch in range(1, CHUNKS) for op in modes for c in range(PASSES)]
+        g_todo = [(g, c, u) for g in range(1, GROUPS) for c in range(PASSES) for u in range(2)]
+        turned = []
+
+        def share(todo, due, s, first):
+            same = [item for item in todo if due(item) == due(todo[0])]
+            if not same or s < first:
+                return []
+            room = max(due(same[0]) - s, 1)
+            picked = same[: -(-len(same) // room)]
+            for item in picked:
+                todo.remove(item)
+            return picked
+
+        def turn(fill, empty, bank):
+            while any(bank is held for held, call in turned):
+                empty_turned(1)
+            fill(bank)
+            turned.append((bank, lambda: empty(bank)))
+
+        def empty_turned(n):
+            for i in range(min(n, len(turned))):
+                turned.pop(0)[1]()
+
+        def x_item(item, bank):
+            turn(lambda bank: x_turn(*item, bank), lambda bank: x_out(*item, bank), bank)
+
+        y_pack = {}
+        for s in range(len(STEPS)):
+            multiply(s, s == last)
+            for u in range(2):
+                if s >= 1:
+                    times_d(s - 1, u, d_banks[s - 1])
+                if s >= 2 and u == 0:
+                    y_quantize(s - 2, y_pack[s - 2])
+                if s >= 1:
+                    add_c(s - 1, u, ADDC[u])
+            empty_turned(len(turned) - 1)
+            for u in range(2):
+                scale_rate(s, u)
+            empty_turned(1)
+            if s == last:
+                break
+            for u in range(2):
+                add_strain(s, u)
+            if s >= 1:
+                y_pack[s - 1] = take("stage", stage)
+                y_interleave(s - 1, y_pack[s - 1])
+            pieces = share(g_todo, lambda item: first_g[item[0]], s, G_FIRST)
+            for item in pieces:
+                if item not in G_SCALAR:
+                    g_piece(*item)
+            quantize_waiting()
+            for item in pieces:
+                if item in G_SCALAR:
+                    g_piece(*item)
+            x_now = share(x_todo, lambda item: first_ch[item[2]] - X_LAG, s, 0)
+            early = x_now if s == 0 else x_now[:1]
+            for i, item in enumerate(early):
+                x_item(item, turn_banks[(i + 2) % 3])
+            if x_now and first_ch[x_now[0][2]] == s + 1:
+                empty_turned(len(turned))
+            if s >= 1:
+                d_turn(s, d_banks[s])
+            if s + 1 == last:
+                d_turn(last, d_banks[last])
+            if s >= 1:
+                for j in tiles(s - 1):
+                    turn(lambda bank: y_turn(s - 1, j, bank, range(PACK)), lambda bank, m=s - 1, j=j: y_copy(m, j, bank), turn_banks[j])
+            for item in x_now[len(early) :]:
+                x_item(item, turn_banks[2])
+            if first_ch[STEPS[s + 1][0] // CHUNK] == s + 1 or first_g[STEPS[s + 1][2]] == s + 1:
+                quantize_waiting()
+
+        add_strain(last, 0)
+        y_pack[last - 1] = take("stage", stage)
+        y_interleave(last - 1, y_pack[last - 1])
+        times_d(last, 0, d_banks[last])
+        add_c(last, 0, TAIL[0])
+        add_strain(last, 1)
+        y_quantize(last - 1, y_pack[last - 1])
+        times_d(last, 1, d_banks[last])
+        for j in tiles(last - 1):
+            y_turn(last - 1, j, turn_banks[j], range(PACK))
+        for j in tiles(last):
+            y_turn(last, j, rate_banks[j], range(2))
+        for j in tiles(last - 1):
+            y_copy(last - 1, j, turn_banks[j])
+        add_c(last, 1, TAIL[1])
+        for j in tiles(last):
+            y_turn(last, j, rate_banks[j], range(2, PACK))
+        y_pack[last] = take("stage", stage)
+        y_interleave(last, y_pack[last])
+        for j in tiles(last):
+            y_copy(last, j, rate_banks[j])
+        y_quantize(last, y_pack[last])

@@ -23,19 +23,26 @@ GROUPS = N // GROUP
 CHUNK = 256
 BANK = 512
 
-X_LAG = 0
+X_COUNT = [4, 3]
 CHUNKS = E // CHUNK
 TILES = CHUNK // P
 PAIRS = sorted([(ch, g) for ch in range(CHUNKS) for g in range(GROUPS)], key=lambda s: (max(2 * s[0], 2 * s[1] + 1), s))
 SPLIT = 0
 G_SCALAR = [(g, c, 1) for g in range(GROUPS) for c in range(PASSES)]
-ADDC = ["GG", "GG"]
-TAIL = ["AA", "VV"]
+ADDC = "GGGA"
+Y_LAG = 2
+I_LAG = 2
+CATCH = 8
+Y_CATCH = 8
+ILV_A = 99
+G_BOTH_FIRST = False
+TAIL = "AAVV"
 WARM = 0
 G_FIRST = 0
-N_WORK = 3
-N_Y = 3
-N_STAGE = 6
+G_LAG = 1
+N_WORK = 4
+N_Y = 4
+N_STAGE = 8
 N_OUT = 8
 
 
@@ -76,7 +83,7 @@ def tile_kelvin_voigt_element_stress_g1_kernel(
         stage = ring("stage", N_STAGE, [P, PACK * CHUNK], BF16)
         y_out = ring("y_out", N_OUT, [P, GROUP], F32)
         y_codes = [sbuf("y_codes%d" % s, [P, w], U32) for s, (e0, w, g) in enumerate(STEPS)]
-        y_scales = ring("y_scales", GROUPS, [P, E], U8)
+        y_scales = sbuf("y_scales", [P, E], U8)
         count = {"turn": 0, "stage": 0, "out": 0}
 
         def take(name, tiles):
@@ -100,7 +107,6 @@ def tile_kelvin_voigt_element_stress_g1_kernel(
 
         first_ch = {ch: min(s for s in range(len(STEPS)) if STEPS[s][0] // CHUNK == ch) for ch in range(CHUNKS)}
         first_g = {g: min(s for s in range(len(STEPS)) if STEPS[s][2] == g) for g in range(GROUPS)}
-        last_g = {g: max(s for s in range(len(STEPS)) if STEPS[s][2] == g) for g in range(GROUPS)}
 
         for s, (e0, w, g) in enumerate(STEPS):
             ch = e0 // CHUNK
@@ -204,12 +210,12 @@ def tile_kelvin_voigt_element_stress_g1_kernel(
             acc = half(s, u).rearrange("p (i e) -> p i e", i=2)
             nc.vector.tensor_tensor(out=acc, in0=pairs, in1=acc, op=ALU.mult)
 
-        def add_c(s, u, engines):
-            for t in (2 * u, 2 * u + 1):
+        def add_c(s, slots, engines):
+            for t in slots:
                 src, dst = work[s % N_WORK][:, slot(s, t)], y_turned[s % N_Y][:, slot(s, t)]
-                if engines[t % 2] == "G":
+                if engines[t] == "G":
                     nc.gpsimd.tensor_scalar(out=dst, in0=src, scalar1=1.0, scalar2=col("c", s, t), op0=ALU.mult, op1=ALU.add)
-                elif engines[t % 2] == "V":
+                elif engines[t] == "V":
                     nc.vector.tensor_scalar(out=dst, in0=src, scalar1=col("c", s, t), scalar2=None, op0=ALU.add)
                 else:
                     nc.scalar.activation(out=dst, in_=src, func=ACT.Identity, bias=col("c", s, t))
@@ -226,8 +232,9 @@ def tile_kelvin_voigt_element_stress_g1_kernel(
             lo = e0 + j * P
             nc.sync.dma_start(out=out_0[lo : lo + P, g * GROUP : (g + 1) * GROUP], in_=dst[:])
 
-        def y_interleave(s, dst):
-            nc.vector.tensor_copy(
+        def y_interleave(s, dst, on_scalar):
+            copy = nc.scalar.copy if on_scalar else nc.vector.tensor_copy
+            copy(
                 out=dst[:, slot(s, 0, PACK)].rearrange("p (a i t) -> p a t i", i=4, t=PACK),
                 in_=y_turned[s % N_Y][:, slot(s, 0, PACK)].rearrange("p (t a i) -> p a t i", t=PACK, i=4),
             )
@@ -235,14 +242,15 @@ def tile_kelvin_voigt_element_stress_g1_kernel(
         def y_quantize(s, src):
             e0, w, g = STEPS[s]
             cols = slice(e0, e0 + w)
-            quantize(y_codes[s][:], y_scales[g][:, cols], src[:, slot(s, 0, PACK)])
+            quantize(y_codes[s][:], y_scales[4 * g :, cols], src[:, slot(s, 0, PACK)])
             words = out_1[g, :, cols, :].rearrange("p m t -> p (m t)").bitcast(I32)
             nc.sync.dma_start(out=words, in_=y_codes[s][:].bitcast(I32))
-            if last_g[g] == s:
+            if s == len(STEPS) - 1:
                 for q in range(4):
-                    nc.sync.dma_start(
-                        out=out_2[g, 4 * q : 4 * q + 4, :].bitcast(I32),
-                        in_=y_scales[g][32 * q : 32 * q + 4, :].bitcast(I32),
+                    queue = nc.scalar if q % 2 else nc.sync
+                    queue.dma_start(
+                        out=out_2[:, 4 * q : 4 * q + 4, :].bitcast(I32),
+                        in_=y_scales[32 * q : 32 * q + 4 * GROUPS, :].bitcast(I32),
                     )
 
         waiting = []
@@ -316,71 +324,104 @@ def tile_kelvin_voigt_element_stress_g1_kernel(
             turn(lambda bank: x_turn(*item, bank), lambda bank: x_out(*item, bank), bank)
 
         y_pack = {}
+
+        def pack(s):
+            y_pack[s] = take("stage", stage)
+            y_interleave(s, y_pack[s], s >= ILV_A)
+
+        def finish(s):
+            for u in range(2):
+                times_d(s, u, d_banks[s])
+                add_c(s, [t for t in (2 * u, 2 * u + 1) if ADDC[t] != "A"], ADDC)
+
+        y_todo = [(s, j) for s in range(len(STEPS)) for j in tiles(s)]
+        pack_todo = list(range(len(STEPS)))
+        packed = []
+
+        def quantize_packed():
+            for m in packed:
+                y_quantize(m, y_pack[m])
+            packed.clear()
+
         for s in range(len(STEPS)):
             multiply(s, s == last)
-            for u in range(2):
-                if s >= 1:
-                    times_d(s - 1, u, d_banks[s - 1])
-                if s >= 2 and u == 0:
-                    y_quantize(s - 2, y_pack[s - 2])
-                if s >= 1:
-                    add_c(s - 1, u, ADDC[u])
+            pieces = share(g_todo, lambda item: first_g[item[0]] - (G_LAG if item[0] > 1 else 0), s, G_FIRST)
+            if s == 1:
+                g_piece(1, 1, 0)
+                quantize_waiting()
+            if s >= 1:
+                finish(s - 1)
             empty_turned(len(turned) - 1)
             for u in range(2):
                 scale_rate(s, u)
             empty_turned(1)
+            for item in pieces:
+                if item in G_SCALAR and s >= 1:
+                    g_piece(*item)
+            if s >= 1:
+                add_c(s - 1, [t for t in range(PACK) if ADDC[t] == "A"], ADDC)
             if s == last:
                 break
             for u in range(2):
                 add_strain(s, u)
-            if s >= 1:
-                y_pack[s - 1] = take("stage", stage)
-                y_interleave(s - 1, y_pack[s - 1])
-            pieces = share(g_todo, lambda item: first_g[item[0]], s, G_FIRST)
+            quantize_packed()
+            lag = I_LAG if s < CATCH else 1
+            for m in [m for m in pack_todo if m <= s - lag]:
+                pack_todo.remove(m)
+                pack(m)
+                packed.append(m)
             for item in pieces:
-                if item not in G_SCALAR:
+                if item not in G_SCALAR and item != (1, 1, 0):
                     g_piece(*item)
-            quantize_waiting()
-            for item in pieces:
-                if item in G_SCALAR:
-                    g_piece(*item)
-            x_now = share(x_todo, lambda item: first_ch[item[2]] - X_LAG, s, 0)
-            early = x_now if s == 0 else x_now[:1]
+            if s > 0:
+                quantize_waiting()
+            x_now = x_todo[: X_COUNT[s] if s < len(X_COUNT) else 1]
+            x_todo = x_todo[len(x_now) :]
+            early = x_now if s < Y_LAG else x_now[:1]
             for i, item in enumerate(early):
                 x_item(item, turn_banks[(i + 2) % 3])
             if x_now and first_ch[x_now[0][2]] == s + 1:
                 empty_turned(len(turned))
+                quantize_waiting()
+            for item in pieces:
+                if item in G_SCALAR and s == 0:
+                    g_piece(*item)
             if s >= 1:
                 d_turn(s, d_banks[s])
-            if s + 1 == last:
-                d_turn(last, d_banks[last])
-            if s >= 1:
-                for j in tiles(s - 1):
-                    turn(lambda bank: y_turn(s - 1, j, bank, range(PACK)), lambda bank, m=s - 1, j=j: y_copy(m, j, bank), turn_banks[j])
+            spare = not x_now and s + 1 < last and s >= Y_CATCH
+            y_now = [item for item in y_todo if item[0] <= s - (1 if s >= Y_CATCH else Y_LAG)][: 3 if spare else 2]
+            for i, item in enumerate(y_now):
+                y_todo.remove(item)
+                turn(lambda bank: y_turn(*item, bank, range(PACK)), lambda bank, item=item: y_copy(*item, bank), turn_banks[i])
             for item in x_now[len(early) :]:
                 x_item(item, turn_banks[2])
-            if first_ch[STEPS[s + 1][0] // CHUNK] == s + 1 or first_g[STEPS[s + 1][2]] == s + 1:
+            if s + 1 == last:
+                empty_turned(len([1 for held, call in turned if held is d_banks[last]]))
+                d_turn(last, d_banks[last])
+            if first_g[STEPS[s + 1][2]] == s + 1:
                 quantize_waiting()
 
+        homes = turn_banks[0:2] + rate_banks
         add_strain(last, 0)
-        y_pack[last - 1] = take("stage", stage)
-        y_interleave(last - 1, y_pack[last - 1])
+        quantize_packed()
+        for m in pack_todo[:-2]:
+            pack(m)
+            packed.append(m)
         times_d(last, 0, d_banks[last])
-        add_c(last, 0, TAIL[0])
+        add_c(last, range(2), TAIL)
         add_strain(last, 1)
-        y_quantize(last - 1, y_pack[last - 1])
+        quantize_packed()
+        pack(last - 1)
         times_d(last, 1, d_banks[last])
-        for j in tiles(last - 1):
-            y_turn(last - 1, j, turn_banks[j], range(PACK))
+        for i, item in enumerate(y_todo[: -len(tiles(last))]):
+            y_turn(*item, homes[i], range(PACK))
+            y_copy(*item, homes[i])
+        y_quantize(last - 1, y_pack[last - 1])
+        add_c(last, range(2, PACK), TAIL)
+        for slots in (range(2), range(2, PACK)):
+            for j in tiles(last):
+                y_turn(last, j, strain_banks[j], slots)
+        pack(last)
         for j in tiles(last):
-            y_turn(last, j, rate_banks[j], range(2))
-        for j in tiles(last - 1):
-            y_copy(last - 1, j, turn_banks[j])
-        add_c(last, 1, TAIL[1])
-        for j in tiles(last):
-            y_turn(last, j, rate_banks[j], range(2, PACK))
-        y_pack[last] = take("stage", stage)
-        y_interleave(last, y_pack[last])
-        for j in tiles(last):
-            y_copy(last, j, rate_banks[j])
+            y_copy(last, j, strain_banks[j])
         y_quantize(last, y_pack[last])

@@ -21,37 +21,24 @@ GROUP = P * PACK
 PASSES = K // GROUP
 GROUPS = N // GROUP
 CHUNK = 256
-BANK = 512
-
-X_COUNT = [4, 3]
 CHUNKS = E // CHUNK
 TILES = CHUNK // P
-PAIRS = sorted([(ch, g) for ch in range(CHUNKS) for g in range(GROUPS)], key=lambda s: (max(2 * s[0], 2 * s[1] + 1), s))
-SPLIT = 0
-G_SCALAR = [(g, c, 1) for g in range(GROUPS) for c in range(PASSES)]
-ADDC = "GGGA"
-Y_LAG = 2
-I_LAG = 2
-CATCH = 8
-Y_CATCH = 8
-ILV_A = 99
-G_BOTH_FIRST = False
-TAIL = "AAVV"
-WARM = 0
-G_FIRST = 0
-G_LAG = 1
-N_WORK = 4
-N_Y = 4
-N_STAGE = 8
-N_OUT = 8
+BANK = 512
+
+STEPS = sorted([(ch, g) for ch in range(CHUNKS) for g in range(GROUPS)], key=lambda s: (max(2 * s[0], 2 * s[1] + 1), s))
+LAST = len(STEPS) - 1
+LAG = 2
+CATCH_UP = 8
+WORK_RING = 4
+PACK_RING = 3
+OUT_RING = 8
+G2_ON_SCALAR = (1,)
 
 
 def tile_kelvin_voigt_element_stress_g1_kernel(
     tc, displacement, velocity, gradient, stiffness, relaxation, prestress, out_0, out_1, out_2
 ):
     nc = tc.nc
-    STEPS = [(ch * CHUNK, CHUNK, g) for ch, g in PAIRS[: len(PAIRS) - SPLIT]]
-    STEPS = STEPS + [(ch * CHUNK + j * P, P, g) for ch, g in PAIRS[len(PAIRS) - SPLIT :] for j in range(TILES)]
     with ExitStack() as ctx:
         sb = ctx.enter_context(tc.tile_pool(name="sb", bufs=1))
         ps = ctx.enter_context(tc.psum_pool(name="ps", bufs=1))
@@ -60,368 +47,309 @@ def tile_kelvin_voigt_element_stress_g1_kernel(
         def sbuf(name, shape, dtype):
             return sb.tile(shape, dtype, name=name, align_bytes=64)
 
-        def ring(name, count, shape, dtype):
-            return [sbuf("%s%d" % (name, i), shape, dtype) for i in range(count)]
+        def ring(name, size, shape, dtype):
+            return [sbuf("%s%d" % (name, i), shape, dtype) for i in range(size)]
 
         banks = [ps.tile([P, BANK], F32, name="bank%d" % i) for i in range(8)]
-        rate_banks, strain_banks, d_bank, turn_banks = banks[0:2], banks[2:4], banks[4], banks[5:8]
+        rate_banks, strain_banks, d_bank, y_banks, x_bank = banks[0:2], banks[2:4], banks[4], banks[5:7], banks[7]
         modes = {"v": velocity, "u": displacement}
 
+        x_keys = [(op, ch) for op in modes for ch in range(CHUNKS)]
         x_raw = {(op, j): sbuf("x_raw_%s%d" % (op, j), [P, K], BF16) for op in modes for j in range(E // P)}
-        x_codes = {(op, c): sbuf("x_codes_%s%d" % (op, c), [P, E], U32) for op in modes for c in range(PASSES)}
-        x_scales = {(op, c): sbuf("x_scales_%s%d" % (op, c), [P, E], U8) for op in modes for c in range(PASSES)}
-        gc = [(g, c) for g in range(GROUPS) for c in range(PASSES)]
-        g_raw = {(g, c): sbuf("g_raw%d%d" % (g, c), [P, PACK, GROUP], BF16) for g, c in gc}
-        g_codes = {(g, c): sbuf("g_codes%d%d" % (g, c), [P, GROUP], U32) for g, c in gc}
-        g_scales = {(g, c): sbuf("g_scales%d%d" % (g, c), [P, GROUP], U8) for g, c in gc}
-        d_raw = [sbuf("d_raw%d" % s, [P, w // P, GROUP], BF16) for s, (e0, w, g) in enumerate(STEPS)]
-        rc_raw = {name: sbuf("raw_" + name, [P, GROUPS, PACK], BF16) for name in ("r", "c")}
-        rc = {name: sbuf("col_" + name, [P, GROUPS * PACK], F32) for name in ("r", "c")}
+        x_stage = {op: ring("x_stage_" + op, PASSES, [P, PACK * CHUNK], BF16) for op in modes}
+        x_codes = {key: sbuf("x_codes_%s%d" % key, [P, PASSES * CHUNK], U32) for key in x_keys}
+        x_scales = {key: sbuf("x_scales_%s%d" % key, [P, PASSES * CHUNK], U8) for key in x_keys}
+        g_keys = [(g, c) for g in range(GROUPS) for c in range(PASSES)]
+        g_raw = {key: sbuf("g_raw%d%d" % key, [P, PACK, GROUP], BF16) for key in g_keys}
+        g_stage = [ring("g_stage%d" % c, 2, [P, PACK * 2 * P], BF16) for c in range(PASSES)]
+        g_codes = {key: sbuf("g_codes%d%d" % key, [P, GROUP], U32) for key in g_keys}
+        g_scales = {key: sbuf("g_scales%d%d" % key, [P, GROUP], U8) for key in g_keys}
+        d_raw = ring("d_raw", len(STEPS), [P, TILES, GROUP], BF16)
+        rc_rows = sbuf("rc_rows", [P, GROUP], BF16)
+        rc_cols = sbuf("rc_cols", [P, 2 * GROUPS, PACK], F32)
         ident = sbuf("ident", [P, P], F32)
-        work = ring("work", N_WORK, [P, PACK * CHUNK], F32)
-        y_turned = ring("y_turned", N_Y, [P, PACK * CHUNK], F32)
-        stage = ring("stage", N_STAGE, [P, PACK * CHUNK], BF16)
-        y_out = ring("y_out", N_OUT, [P, GROUP], F32)
-        y_codes = [sbuf("y_codes%d" % s, [P, w], U32) for s, (e0, w, g) in enumerate(STEPS)]
+        work = ring("work", WORK_RING, [P, 2 * BANK], F32)
+        y_slots = ring("y_slots", WORK_RING, [P, 2 * BANK], F32)
+        y_packed = ring("y_packed", PACK_RING, [P, PACK * CHUNK], BF16)
+        y_out = ring("y_out", OUT_RING, [P, GROUP], F32)
+        y_codes = ring("y_codes", len(STEPS), [P, CHUNK], U32)
         y_scales = sbuf("y_scales", [P, E], U8)
-        count = {"turn": 0, "stage": 0, "out": 0}
 
-        def take(name, tiles):
-            count[name] = count[name] + 1
-            return tiles[(count[name] - 1) % len(tiles)]
-
+        nc.vector.memset(rc_rows[:].bitcast(I32), 0)
         make_identity(nc, ident[:])
 
-        def load_x(op, ch):
-            for j in range(ch * TILES, (ch + 1) * TILES):
-                nc.sync.dma_start(out=x_raw[op, j][:], in_=modes[op][j * P : (j + 1) * P, :])
-
-        def load_g(g, c):
-            rows = gradient[c * GROUP : (c + 1) * GROUP, g * GROUP : (g + 1) * GROUP]
-            nc.sync.dma_start(out=g_raw[g, c][:], in_=rows.rearrange("(p j) n -> p j n", j=PACK))
-
         def load_d(s):
-            e0, w, g = STEPS[s]
-            rows = stiffness[e0 : e0 + w, g * GROUP : (g + 1) * GROUP]
+            ch, g = STEPS[s]
+            rows = stiffness[ch * CHUNK : (ch + 1) * CHUNK, g * GROUP : (g + 1) * GROUP]
             nc.sync.dma_start(out=d_raw[s][:], in_=rows.rearrange("(j p) n -> p j n", p=P))
 
-        first_ch = {ch: min(s for s in range(len(STEPS)) if STEPS[s][0] // CHUNK == ch) for ch in range(CHUNKS)}
-        first_g = {g: min(s for s in range(len(STEPS)) if STEPS[s][2] == g) for g in range(GROUPS)}
-
-        for s, (e0, w, g) in enumerate(STEPS):
-            ch = e0 // CHUNK
+        first_ch = [min(s for s, step in enumerate(STEPS) if step[0] == ch) for ch in range(CHUNKS)]
+        first_g = [min(s for s, step in enumerate(STEPS) if step[1] == g) for g in range(GROUPS)]
+        for s, (ch, g) in enumerate(STEPS):
             for c, op in enumerate(modes):
                 if first_ch[ch] == s:
-                    load_x(op, ch)
+                    for j in range(ch * TILES, (ch + 1) * TILES):
+                        nc.sync.dma_start(out=x_raw[op, j][:], in_=modes[op][j * P : (j + 1) * P, :])
                 if first_g[g] == s:
-                    load_g(g, c)
+                    rows = gradient[c * GROUP : (c + 1) * GROUP, g * GROUP : (g + 1) * GROUP]
+                    nc.sync.dma_start(out=g_raw[g, c][:], in_=rows.rearrange("(p j) n -> p j n", j=PACK))
             if s == 0:
-                for name, vec in (("r", relaxation), ("c", prestress)):
-                    nc.sync.dma_start(out=rc_raw[name][:], in_=vec.rearrange("(g p t) -> p g t", p=P, t=PACK))
-            load_d(s)
+                for i, vec in enumerate((relaxation, prestress)):
+                    rows = vec.rearrange("(g n) -> g n", n=GROUP)
+                    nc.sync.dma_start(out=rc_rows[i * GROUPS : (i + 1) * GROUPS, :], in_=rows)
+            else:
+                load_d(s - 1)
+        load_d(LAST)
 
         def quantize(codes, scales, src):
             nc.vector.quantize_mx(out=codes.bitcast(FP8X4), scales=scales, in_=src)
 
-        def g_interleave(g, c, u, dst, on_scalar):
-            src = g_raw[g, c][:].rearrange("p j (a b t) -> p a t b j", b=2, t=PACK)[:, :, 2 * u : 2 * u + 2, :, :]
-            out = dst[:].rearrange("p (t a b j) -> p a t b j", t=2, b=2, j=PACK)
-            if on_scalar:
-                nc.scalar.copy(out=out, in_=src)
-            else:
-                nc.vector.tensor_copy(out=out, in_=src)
+        def turn_pairs(bank, col0, width, rows):
+            pairs = rows.bitcast(F32)
+            for u in range(2):
+                lo = u * width + col0
+                nc.tensor.transpose(bank[:, lo : lo + P], pairs[:, u::2], ident[:])
 
-        def g_quantize(g, c, u, src):
+        staged = []
+
+        def quantize_staged(keep=0):
+            while len(staged) > keep:
+                quantize(*staged.pop(0))
+
+        def g_half(g, c, u, copy):
+            dst = g_stage[c][u]
+            src = g_raw[g, c][:].rearrange("p j (a b t) -> p a j b t", b=2, t=PACK)[:, :, :, :, 2 * u : 2 * u + 2]
+            copy(out=dst[:].rearrange("p (t a b j) -> p a j b t", t=2, b=2, j=PACK), in_=src)
             cols = slice(2 * u * P, 2 * (u + 1) * P)
-            quantize(g_codes[g, c][:, cols], g_scales[g, c][:, cols], src[:])
+            staged.append((g_codes[g, c][:, cols], g_scales[g, c][:, cols], dst[:]))
 
         def x_turn(op, c, ch, bank):
-            for i in range(TILES):
-                words = x_raw[op, ch * TILES + i][:].bitcast(F32)
-                for u in range(2):
-                    nc.tensor.transpose(
-                        bank[:, u * CHUNK + i * P : u * CHUNK + (i + 1) * P],
-                        words[:, 256 * c + u : 256 * (c + 1) : 2],
-                        ident[:],
-                    )
+            for j in range(TILES):
+                turn_pairs(bank, j * P, CHUNK, x_raw[op, ch * TILES + j][:, c * GROUP : (c + 1) * GROUP])
 
-        def x_copy(bank, dst):
+        def x_out(op, c, ch, bank):
+            dst = x_stage[op][c]
             nc.scalar.copy(
                 out=dst[:].bitcast(F32).rearrange("p (e u) -> p e u", u=2),
                 in_=bank[:].rearrange("p (u e) -> p e u", u=2),
             )
+            cols = slice(c * CHUNK, (c + 1) * CHUNK)
+            staged.append((x_codes[op, ch][:, cols], x_scales[op, ch][:, cols], dst[:]))
 
-        def x_quantize(op, c, ch, src):
-            cols = slice(ch * CHUNK, (ch + 1) * CHUNK)
-            quantize(x_codes[op, c][:, cols], x_scales[op, c][:, cols], src[:])
+        def runs(s, h):
+            if s == LAST:
+                return [(t, h * P, P) for t in range(PACK)]
+            return [(t, 0, CHUNK) for t in (2 * h, 2 * h + 1)]
 
-        def slot(s, t, n=1):
-            return slice(t * STEPS[s][1], (t + n) * STEPS[s][1])
-
-        def tiles(s):
-            return range(STEPS[s][1] // P)
-
-        def multiply(s, by_pair):
-            e0, w, g = STEPS[s]
-            cols = slice(e0, e0 + w)
-            order = [(op, pair, u) for op, pair in (("v", rate_banks), ("u", strain_banks)) for u in range(2)]
-            if by_pair:
-                order = sorted(order, key=lambda item: item[2])
-            for op, pair, u in order:
-                for t in (2 * u, 2 * u + 1):
-                    for c in range(PASSES):
-                        nc.tensor.matmul_mx(
-                            out=pair[t // 2][:, slot(s, t % 2)],
-                            lhsT=g_codes[g, c][:, t * P : (t + 1) * P].bitcast(FP8X4),
-                            lhsT_scale=g_scales[g, c][:, t * P : (t + 1) * P],
-                            rhs=x_codes[op, c][:, cols].bitcast(FP8X4),
-                            rhs_scale=x_scales[op, c][:, cols],
-                            start=(c == 0),
-                            stop=(c == PASSES - 1),
-                        )
-
-        def col(name, s, t):
-            i = STEPS[s][2] * PACK + t
-            return rc[name][:, i : i + 1]
-
-        def half(s, u):
-            return work[s % N_WORK][:, slot(s, 2 * u, 2)]
-
-        def scale_rate(s, u):
-            for t in (2 * u, 2 * u + 1):
-                nc.scalar.activation(
-                    out=work[s % N_WORK][:, slot(s, t)], in_=rate_banks[u][:, slot(s, t % 2)], func=ACT.Copy, scale=col("r", s, t)
-                )
-
-        def add_strain(s, u):
-            nc.vector.tensor_tensor(out=half(s, u), in0=strain_banks[u][:, slot(s, 0, 2)], in1=half(s, u), op=ALU.add)
-
-        def d_turn(s, bank):
-            w = STEPS[s][1]
-            for j in range(w // P):
-                words = d_raw[s][:, j, :].bitcast(F32)
-                for u in range(2):
-                    nc.tensor.transpose(
-                        bank[:, u * w + j * P : u * w + (j + 1) * P], words[:, u : GROUP // 2 : 2], ident[:]
-                    )
-
-        def times_d(s, u, bank):
-            pairs = bank[:, slot(s, u)].bitcast(BF16).rearrange("p (e i) -> p i e", i=2)
-            acc = half(s, u).rearrange("p (i e) -> p i e", i=2)
-            nc.vector.tensor_tensor(out=acc, in0=pairs, in1=acc, op=ALU.mult)
-
-        def add_c(s, slots, engines):
-            for t in slots:
-                src, dst = work[s % N_WORK][:, slot(s, t)], y_turned[s % N_Y][:, slot(s, t)]
-                if engines[t] == "G":
-                    nc.gpsimd.tensor_scalar(out=dst, in0=src, scalar1=1.0, scalar2=col("c", s, t), op0=ALU.mult, op1=ALU.add)
-                elif engines[t] == "V":
-                    nc.vector.tensor_scalar(out=dst, in0=src, scalar1=col("c", s, t), scalar2=None, op0=ALU.add)
-                else:
-                    nc.scalar.activation(out=dst, in_=src, func=ACT.Identity, bias=col("c", s, t))
-
-        def y_turn(s, j, bank, slots):
-            for t in slots:
-                lo = t * STEPS[s][1] + j * P
-                nc.tensor.transpose(bank[:, t * P : (t + 1) * P], y_turned[s % N_Y][:, lo : lo + P], ident[:])
-
-        def y_copy(s, j, bank):
-            e0, w, g = STEPS[s]
-            dst = take("out", y_out)
-            nc.scalar.copy(out=dst[:].rearrange("e (p t) -> e p t", t=PACK), in_=bank[:].rearrange("e (t p) -> e p t", t=PACK))
-            lo = e0 + j * P
-            nc.sync.dma_start(out=out_0[lo : lo + P, g * GROUP : (g + 1) * GROUP], in_=dst[:])
-
-        def y_interleave(s, dst, on_scalar):
-            copy = nc.scalar.copy if on_scalar else nc.vector.tensor_copy
-            copy(
-                out=dst[:, slot(s, 0, PACK)].rearrange("p (a i t) -> p a t i", i=4, t=PACK),
-                in_=y_turned[s % N_Y][:, slot(s, 0, PACK)].rearrange("p (t a i) -> p a t i", t=PACK, i=4),
+        def mx(out, g, t, op, ch, c, e0, w, start, stop):
+            x_cols = slice(c * CHUNK + e0, c * CHUNK + e0 + w)
+            nc.tensor.matmul_mx(
+                out=out,
+                lhsT=g_codes[g, c][:, t * P : (t + 1) * P].bitcast(FP8X4),
+                lhsT_scale=g_scales[g, c][:, t * P : (t + 1) * P],
+                rhs=x_codes[op, ch][:, x_cols].bitcast(FP8X4),
+                rhs_scale=x_scales[op, ch][:, x_cols],
+                start=start,
+                stop=stop,
             )
 
-        def y_quantize(s, src):
-            e0, w, g = STEPS[s]
-            cols = slice(e0, e0 + w)
-            quantize(y_codes[s][:], y_scales[4 * g :, cols], src[:, slot(s, 0, PACK)])
-            words = out_1[g, :, cols, :].rearrange("p m t -> p (m t)").bitcast(I32)
-            nc.sync.dma_start(out=words, in_=y_codes[s][:].bitcast(I32))
-            if s == len(STEPS) - 1:
-                for q in range(4):
-                    queue = nc.scalar if q % 2 else nc.sync
-                    queue.dma_start(
-                        out=out_2[:, 4 * q : 4 * q + 4, :].bitcast(I32),
-                        in_=y_scales[32 * q : 32 * q + 4 * GROUPS, :].bitcast(I32),
-                    )
+        def multiply(s):
+            ch, g = STEPS[s]
+            order = [(op, pair, h) for op, pair in (("v", rate_banks), ("u", strain_banks)) for h in range(2)]
+            if s in (0, LAST):
+                order = sorted(order, key=lambda item: item[2])
+            for op, pair, h in order:
+                for i, (t, e0, w) in enumerate(runs(s, h)):
+                    for c in range(PASSES):
+                        mx(pair[h][:, i * w : (i + 1) * w], g, t, op, ch, c, e0, w, c == 0, c == PASSES - 1)
 
-        waiting = []
+        def half(s, h):
+            return work[s % WORK_RING][:, h * BANK : (h + 1) * BANK]
 
-        def quantize_waiting(keep=0):
-            while len(waiting) > keep:
-                waiting.pop(0)()
+        def scale_rate(s, h):
+            for i, (t, e0, w) in enumerate(runs(s, h)):
+                cols = slice(i * w, (i + 1) * w)
+                r_col = rc_cols[:, STEPS[s][1], t : t + 1]
+                nc.scalar.activation(out=half(s, h)[:, cols], in_=rate_banks[h][:, cols], func=ACT.Copy, scale=r_col)
 
-        def g_piece(g, c, u):
-            dst = take("stage", stage)
-            g_interleave(g, c, u, dst, (g, c, u) in G_SCALAR)
-            waiting.append(lambda: g_quantize(g, c, u, dst))
+        def add_strain(s, h):
+            nc.vector.tensor_tensor(out=half(s, h), in0=strain_banks[h][:], in1=half(s, h), op=ALU.add)
 
-        def x_out(op, c, ch, bank):
-            dst = take("stage", stage)
-            x_copy(bank, dst)
-            waiting.append(lambda: x_quantize(op, c, ch, dst))
+        def d_turn(s, bank):
+            for j in range(TILES):
+                turn_pairs(bank, j * P, CHUNK, d_raw[s][:, j, :])
+
+        def times_d(s, h, bank):
+            if s == LAST:
+                d_t = bank[:].bitcast(BF16).rearrange("p (u j e i) -> p j u i e", u=2, j=TILES, i=2)[:, h, :, :, :]
+                acc = half(s, h).rearrange("p (u i e) -> p u i e", u=2, i=2)
+            else:
+                d_t = bank[:, h * CHUNK : (h + 1) * CHUNK].bitcast(BF16).rearrange("p (e i) -> p i e", i=2)
+                acc = half(s, h).rearrange("p (i e) -> p i e", i=2)
+            nc.vector.tensor_tensor(out=acc, in0=d_t, in1=acc, op=ALU.mult)
+
+        def add_c(s, h, i, engine):
+            t, e0, w = runs(s, h)[i]
+            cols = slice(h * BANK + i * w, h * BANK + (i + 1) * w)
+            src, dst = work[s % WORK_RING][:, cols], y_slots[s % WORK_RING][:, cols]
+            c_col = rc_cols[:, GROUPS + STEPS[s][1], t : t + 1]
+            if engine is nc.scalar:
+                nc.scalar.activation(out=dst, in_=src, func=ACT.Identity, bias=c_col)
+            else:
+                engine.tensor_scalar(out=dst, in0=src, scalar1=1.0, scalar2=c_col, op0=ALU.mult, op1=ALU.add)
+
+        def y_turn(s, j, bank):
+            for t in range(PACK):
+                lo = (j * PACK + t) * P if s == LAST else t * CHUNK + j * P
+                nc.tensor.transpose(bank[:, t * P : (t + 1) * P], y_slots[s % WORK_RING][:, lo : lo + P], ident[:])
+
+        def y_store(s, j, bank):
+            ch, g = STEPS[s]
+            dst = y_out[(s * TILES + j) % OUT_RING]
+            nc.scalar.copy(
+                out=dst[:].rearrange("e (p t) -> e p t", t=PACK),
+                in_=bank[:].rearrange("e (t p) -> e p t", t=PACK),
+            )
+            lo = ch * CHUNK + j * P
+            nc.sync.dma_start(out=out_0[lo : lo + P, g * GROUP : (g + 1) * GROUP], in_=dst[:])
+
+        packed = []
+
+        def y_pack(s, e0, w):
+            cols = slice(PACK * e0, PACK * (e0 + w))
+            nc.vector.tensor_copy(
+                out=y_packed[s % PACK_RING][:, cols].rearrange("p (a i t) -> p a t i", i=4, t=PACK),
+                in_=y_slots[s % WORK_RING][:, cols].rearrange("p (t a i) -> p a t i", t=PACK, i=4),
+            )
+            packed.append((s, e0, w))
+
+        def quantize_packed():
+            while packed:
+                s, e0, w = packed.pop(0)
+                ch, g = STEPS[s]
+                lo = ch * CHUNK
+                src = y_packed[s % PACK_RING][:, PACK * e0 : PACK * (e0 + w)]
+                quantize(y_codes[s][:, e0 : e0 + w], y_scales[4 * g :, lo + e0 : lo + e0 + w], src)
+                if e0 + w == CHUNK:
+                    words = out_1[g, :, lo : lo + CHUNK, :].rearrange("p m t -> p (m t)").bitcast(I32)
+                    nc.sync.dma_start(out=words, in_=y_codes[s][:].bitcast(I32))
+
+        turned = []
+
+        def empty_turned(keep=0):
+            while len(turned) > keep:
+                bank, empty, item = turned.pop(0)
+                empty(*item, bank)
+
+        def free(bank):
+            while any(bank is entry[0] for entry in turned):
+                empty_turned(keep=len(turned) - 1)
+
+        def turn(fill, empty, item, bank):
+            free(bank)
+            fill(*item, bank)
+            turned.append((bank, empty, item))
 
         for i, op in enumerate(modes):
             for c in range(PASSES):
                 x_turn(op, c, 0, banks[PASSES * i + c])
             x_out(op, 0, 0, banks[PASSES * i])
-            quantize_waiting(keep=1)
-            g_piece(0, i, 0)
+            quantize_staged(keep=1)
+            g_half(0, i, 0, nc.vector.tensor_copy)
             x_out(op, 1, 0, banks[PASSES * i + 1])
-            g_piece(0, i, 1)
-        quantize_waiting(keep=1)
-        for name in ("r", "c"):
-            nc.vector.tensor_copy(out=rc[name][:], in_=rc_raw[name][:].rearrange("p g t -> p (g t)"))
-        quantize_waiting()
-        for i in range(WARM):
-            nc.tensor.matmul_mx(
-                out=turn_banks[0][:, 0:CHUNK],
-                lhsT=g_codes[0, 0][:, 0:P].bitcast(FP8X4),
-                lhsT_scale=g_scales[0, 0][:, 0:P],
-                rhs=x_codes["v", 0][:, 0:CHUNK].bitcast(FP8X4),
-                rhs_scale=x_scales["v", 0][:, 0:CHUNK],
-                start=True,
-                stop=True,
-            )
-        last = len(STEPS) - 1
-        d_banks = {s: d_bank for s in range(last)}
-        d_banks[last] = turn_banks[2]
-        d_turn(0, d_banks[0])
+            g_half(0, i, 1, nc.scalar.copy)
+        quantize_staged(keep=1)
+        turn_pairs(d_bank, 0, P, rc_rows[:])
+        rc_pairs = d_bank[:, 0 : 2 * P].bitcast(BF16).rearrange("p (u r i) -> p u r i", u=2, i=2)
+        nc.vector.tensor_copy(out=rc_cols[:].rearrange("p r (u i) -> p u r i", u=2), in_=rc_pairs[:, :, 0 : 2 * GROUPS, :])
+        quantize_staged()
 
         x_todo = [(op, c, ch) for ch in range(1, CHUNKS) for op in modes for c in range(PASSES)]
-        g_todo = [(g, c, u) for g in range(1, GROUPS) for c in range(PASSES) for u in range(2)]
-        turned = []
-
-        def share(todo, due, s, first):
-            same = [item for item in todo if due(item) == due(todo[0])]
-            if not same or s < first:
-                return []
-            room = max(due(same[0]) - s, 1)
-            picked = same[: -(-len(same) // room)]
-            for item in picked:
-                todo.remove(item)
-            return picked
-
-        def turn(fill, empty, bank):
-            while any(bank is held for held, call in turned):
-                empty_turned(1)
-            fill(bank)
-            turned.append((bank, lambda: empty(bank)))
-
-        def empty_turned(n):
-            for i in range(min(n, len(turned))):
-                turned.pop(0)[1]()
-
-        def x_item(item, bank):
-            turn(lambda bank: x_turn(*item, bank), lambda bank: x_out(*item, bank), bank)
-
-        y_pack = {}
-
-        def pack(s):
-            y_pack[s] = take("stage", stage)
-            y_interleave(s, y_pack[s], s >= ILV_A)
-
-        def finish(s):
-            for u in range(2):
-                times_d(s, u, d_banks[s])
-                add_c(s, [t for t in (2 * u, 2 * u + 1) if ADDC[t] != "A"], ADDC)
-
-        y_todo = [(s, j) for s in range(len(STEPS)) for j in tiles(s)]
-        pack_todo = list(range(len(STEPS)))
-        packed = []
-
-        def quantize_packed():
-            for m in packed:
-                y_quantize(m, y_pack[m])
-            packed.clear()
+        g2_halves = [(2, c, u) for c in range(PASSES) for u in range(2)]
+        g2_plan = {1 + i: item for i, item in enumerate(g2_halves)}
+        y_todo = [(s, j) for s in range(LAST) for j in range(TILES)]
+        pack_todo = list(range(LAST))
 
         for s in range(len(STEPS)):
-            multiply(s, s == last)
-            pieces = share(g_todo, lambda item: first_g[item[0]] - (G_LAG if item[0] > 1 else 0), s, G_FIRST)
+            multiply(s)
             if s == 1:
-                g_piece(1, 1, 0)
-                quantize_waiting()
+                g_half(1, 1, 0, nc.vector.tensor_copy)
+                quantize_staged()
             if s >= 1:
-                finish(s - 1)
-            empty_turned(len(turned) - 1)
-            for u in range(2):
-                scale_rate(s, u)
-            empty_turned(1)
-            for item in pieces:
-                if item in G_SCALAR and s >= 1:
-                    g_piece(*item)
-            if s >= 1:
-                add_c(s - 1, [t for t in range(PACK) if ADDC[t] == "A"], ADDC)
-            if s == last:
+                for h in range(2):
+                    times_d(s - 1, h, d_bank)
+                    for i in range(2 - h):
+                        add_c(s - 1, h, i, nc.gpsimd)
+            empty_turned(keep=1)
+            scale_rate(s, 0)
+            if s == LAST:
                 break
-            for u in range(2):
-                add_strain(s, u)
-            quantize_packed()
-            lag = I_LAG if s < CATCH else 1
-            for m in [m for m in pack_todo if m <= s - lag]:
-                pack_todo.remove(m)
-                pack(m)
-                packed.append(m)
-            for item in pieces:
-                if item not in G_SCALAR and item != (1, 1, 0):
-                    g_piece(*item)
-            if s > 0:
-                quantize_waiting()
-            x_now = x_todo[: X_COUNT[s] if s < len(X_COUNT) else 1]
-            x_todo = x_todo[len(x_now) :]
-            early = x_now if s < Y_LAG else x_now[:1]
-            for i, item in enumerate(early):
-                x_item(item, turn_banks[(i + 2) % 3])
-            if x_now and first_ch[x_now[0][2]] == s + 1:
-                empty_turned(len(turned))
-                quantize_waiting()
-            for item in pieces:
-                if item in G_SCALAR and s == 0:
-                    g_piece(*item)
+            scale_rate(s, 1)
+            empty_turned()
+            if s == 1:
+                g_half(1, 1, 1, nc.scalar.copy)
+            if s in g2_plan and g2_plan[s][2] in G2_ON_SCALAR:
+                g_half(*g2_plan[s], nc.scalar.copy)
             if s >= 1:
-                d_turn(s, d_banks[s])
-            spare = not x_now and s + 1 < last and s >= Y_CATCH
-            y_now = [item for item in y_todo if item[0] <= s - (1 if s >= Y_CATCH else Y_LAG)][: 3 if spare else 2]
-            for i, item in enumerate(y_now):
-                y_todo.remove(item)
-                turn(lambda bank: y_turn(*item, bank, range(PACK)), lambda bank, item=item: y_copy(*item, bank), turn_banks[i])
-            for item in x_now[len(early) :]:
-                x_item(item, turn_banks[2])
-            if s + 1 == last:
-                empty_turned(len([1 for held, call in turned if held is d_banks[last]]))
-                d_turn(last, d_banks[last])
-            if first_g[STEPS[s + 1][2]] == s + 1:
-                quantize_waiting()
+                add_c(s - 1, 1, 1, nc.scalar)
+            for h in range(2):
+                add_strain(s, h)
+            quantize_packed()
+            lag = LAG if s < CATCH_UP else 1
+            while pack_todo and pack_todo[0] <= s - lag:
+                y_pack(pack_todo.pop(0), 0, CHUNK)
+            if s in g2_plan and g2_plan[s][2] not in G2_ON_SCALAR:
+                g_half(*g2_plan[s], nc.vector.tensor_copy)
+            if s == 0:
+                g_half(1, 0, 0, nc.vector.tensor_copy)
+                for bank in [x_bank] + y_banks + [x_bank]:
+                    turn(x_turn, x_out, x_todo.pop(0), bank)
+                empty_turned()
+                quantize_staged()
+                g_half(1, 0, 1, nc.scalar.copy)
+                d_turn(0, d_bank)
+                continue
+            quantize_staged()
+            x_banks = [x_bank] if s >= LAG else [x_bank] + y_banks
+            y_room = y_banks if x_todo or s + 1 == LAST else y_banks + [x_bank]
+            for bank in x_banks[: len(x_todo)]:
+                turn(x_turn, x_out, x_todo.pop(0), bank)
+            d_turn(s, d_bank)
+            for bank in y_room:
+                if y_todo[0][0] <= s - lag:
+                    turn(y_turn, y_store, y_todo.pop(0), bank)
+            if s + 1 == LAST:
+                free(x_bank)
+                d_turn(LAST, x_bank)
 
-        homes = turn_banks[0:2] + rate_banks
-        add_strain(last, 0)
+        add_c(LAST - 1, 1, 1, nc.scalar)
+        empty_turned()
+        scale_rate(LAST, 1)
+        add_strain(LAST, 0)
         quantize_packed()
-        for m in pack_todo[:-2]:
-            pack(m)
-            packed.append(m)
-        times_d(last, 0, d_banks[last])
-        add_c(last, range(2), TAIL)
-        add_strain(last, 1)
+        y_pack(LAST - 1, 0, CHUNK)
+        times_d(LAST, 0, x_bank)
+        for j in range(TILES):
+            y_turn(LAST - 1, j, y_banks[j])
+        y_store(LAST - 1, 0, y_banks[0])
+        for i in range(PACK):
+            add_c(LAST, 0, i, nc.scalar)
+        add_strain(LAST, 1)
         quantize_packed()
-        pack(last - 1)
-        times_d(last, 1, d_banks[last])
-        for i, item in enumerate(y_todo[: -len(tiles(last))]):
-            y_turn(*item, homes[i], range(PACK))
-            y_copy(*item, homes[i])
-        y_quantize(last - 1, y_pack[last - 1])
-        add_c(last, range(2, PACK), TAIL)
-        for slots in (range(2), range(2, PACK)):
-            for j in tiles(last):
-                y_turn(last, j, strain_banks[j], slots)
-        pack(last)
-        for j in tiles(last):
-            y_copy(last, j, strain_banks[j])
-        y_quantize(last, y_pack[last])
+        times_d(LAST, 1, x_bank)
+        y_store(LAST - 1, 1, y_banks[1])
+        y_pack(LAST, 0, P)
+        for i in range(PACK):
+            add_c(LAST, 1, i, nc.vector)
+        quantize_packed()
+        for j in range(TILES):
+            y_turn(LAST, j, rate_banks[j])
+            y_store(LAST, j, rate_banks[j])
+        y_pack(LAST, P, P)
+        quantize_packed()
+        for q in range(4):
+            queue = nc.scalar if q % 2 else nc.sync
+            queue.dma_start(
+                out=out_2[:, 4 * q : 4 * q + 4, :].bitcast(I32),
+                in_=y_scales[32 * q : 32 * q + 4 * GROUPS, :].bitcast(I32),
+            )

@@ -32,7 +32,6 @@ CATCH_UP = 8
 WORK_RING = 4
 PACK_RING = 3
 OUT_RING = 8
-G2_ON_SCALAR = (1,)
 
 
 def tile_kelvin_voigt_element_stress_g1_kernel(
@@ -278,7 +277,7 @@ def tile_kelvin_voigt_element_stress_g1_kernel(
             if s >= 1:
                 for h in range(2):
                     times_d(s - 1, h, d_bank)
-                    for i in range(2 - h):
+                    for i in range(2 - h if s < LAST else 0):
                         add_c(s - 1, h, i, nc.gpsimd)
             empty_turned(keep=1)
             scale_rate(s, 0)
@@ -288,28 +287,30 @@ def tile_kelvin_voigt_element_stress_g1_kernel(
             empty_turned()
             if s == 1:
                 g_half(1, 1, 1, nc.scalar.copy)
-            if s in g2_plan and g2_plan[s][2] in G2_ON_SCALAR:
+            if s in g2_plan and g2_plan[s][2] == 1:
                 g_half(*g2_plan[s], nc.scalar.copy)
             if s >= 1:
                 add_c(s - 1, 1, 1, nc.scalar)
             for h in range(2):
                 add_strain(s, h)
             quantize_packed()
+            quantize_staged()
             lag = LAG if s < CATCH_UP else 1
             while pack_todo and pack_todo[0] <= s - lag:
                 y_pack(pack_todo.pop(0), 0, CHUNK)
-            if s in g2_plan and g2_plan[s][2] not in G2_ON_SCALAR:
+            if s in g2_plan and g2_plan[s][2] == 0:
                 g_half(*g2_plan[s], nc.vector.tensor_copy)
             if s == 0:
                 g_half(1, 0, 0, nc.vector.tensor_copy)
+                not_yet = staged.pop()
                 for bank in [x_bank] + y_banks + [x_bank]:
                     turn(x_turn, x_out, x_todo.pop(0), bank)
                 empty_turned()
                 quantize_staged()
+                staged.append(not_yet)
                 g_half(1, 0, 1, nc.scalar.copy)
                 d_turn(0, d_bank)
                 continue
-            quantize_staged()
             x_banks = [x_bank] if s >= LAG else [x_bank] + y_banks
             y_room = y_banks if x_todo or s + 1 == LAST else y_banks + [x_bank]
             for bank in x_banks[: len(x_todo)]:
@@ -322,11 +323,13 @@ def tile_kelvin_voigt_element_stress_g1_kernel(
                 free(x_bank)
                 d_turn(LAST, x_bank)
 
-        add_c(LAST - 1, 1, 1, nc.scalar)
+        quantize_packed()
+        for h in range(2):
+            for i in range(2):
+                add_c(LAST - 1, h, i, nc.vector)
         empty_turned()
         scale_rate(LAST, 1)
         add_strain(LAST, 0)
-        quantize_packed()
         y_pack(LAST - 1, 0, CHUNK)
         times_d(LAST, 0, x_bank)
         for j in range(TILES):
@@ -340,13 +343,14 @@ def tile_kelvin_voigt_element_stress_g1_kernel(
         y_store(LAST - 1, 1, y_banks[1])
         y_pack(LAST, 0, P)
         for i in range(PACK):
-            add_c(LAST, 1, i, nc.vector)
+            add_c(LAST, 1, i, nc.scalar if i < 2 else nc.vector)
         quantize_packed()
         for j in range(TILES):
             y_turn(LAST, j, rate_banks[j])
-            y_store(LAST, j, rate_banks[j])
+        y_store(LAST, 0, rate_banks[0])
         y_pack(LAST, P, P)
         quantize_packed()
+        y_store(LAST, 1, rate_banks[1])
         for q in range(4):
             queue = nc.scalar if q % 2 else nc.sync
             queue.dma_start(

@@ -29,6 +29,7 @@ STEPS = sorted([(ch, g) for ch in range(CHUNKS) for g in range(GROUPS)], key=lam
 LAST = len(STEPS) - 1
 LAG = 2
 CATCH_UP = 8
+WARM_UP = 4
 WORK_RING = 4
 PACK_RING = 3
 OUT_RING = 8
@@ -258,6 +259,8 @@ def tile_kelvin_voigt_element_stress_g1_kernel(
             x_out(op, 1, 0, banks[PASSES * i + 1])
             g_half(0, i, 1, nc.scalar.copy)
         quantize_staged(keep=1)
+        for i in range(WARM_UP):
+            mx(y_banks[0][:, 0:CHUNK], 0, 0, "v", 0, 0, 0, CHUNK, True, True)
         turn_pairs(d_bank, 0, P, rc_rows[:])
         rc_pairs = d_bank[:, 0 : 2 * P].bitcast(BF16).rearrange("p (u r i) -> p u r i", u=2, i=2)
         nc.vector.tensor_copy(out=rc_cols[:].rearrange("p r (u i) -> p u r i", u=2), in_=rc_pairs[:, :, 0 : 2 * GROUPS, :])

from contextlib import ExitStack

import concourse.mybir as mybir
from concourse.masks import make_identity

E, K, N = 1024, 1024, 1536
FLOPS = 2 * 2 * E * K * N

F32 = mybir.dt.float32
BF16 = mybir.dt.bfloat16
U32 = mybir.dt.uint32
I32 = mybir.dt.int32
U8 = mybir.dt.uint8
FP8X4 = mybir.dt.float8_e4m3fn_x4
ALU = mybir.AluOpType
ACT = mybir.ActivationFunctionType

P = 128
PACK = 4
GROUP = P * PACK
PASSES = K // GROUP
GROUPS = N // GROUP
CHUNK = 256
CHUNKS = E // CHUNK
TILES = CHUNK // P
BANK = 512

STEPS = sorted([(ch, g) for ch in range(CHUNKS) for g in range(GROUPS)], key=lambda s: (max(2 * s[0], 2 * s[1] + 1), s))
LAST = len(STEPS) - 1
LAG = 2
CATCH_UP = 8
WARM_UP = 4
WORK_RING = 4
PACK_RING = 3
OUT_RING = 8


def tile_kelvin_voigt_element_stress_g1_kernel(
    tc, displacement, velocity, gradient, stiffness, relaxation, prestress, out_0, out_1, out_2
):
    nc = tc.nc
    with ExitStack() as ctx:
        sb = ctx.enter_context(tc.tile_pool(name="sb", bufs=1))
        ps = ctx.enter_context(tc.psum_pool(name="ps", bufs=1))
        ctx.enter_context(tc.manual_schedule())

        def sbuf(name, shape, dtype):
            return sb.tile(shape, dtype, name=name, align_bytes=64)

        def ring(name, size, shape, dtype):
            return [sbuf("%s%d" % (name, i), shape, dtype) for i in range(size)]

        banks = [ps.tile([P, BANK], F32, name="bank%d" % i) for i in range(8)]
        rate_banks, strain_banks, d_bank, y_banks, x_bank = banks[0:2], banks[2:4], banks[4], banks[5:7], banks[7]
        modes = {"v": velocity, "u": displacement}

        x_keys = [(op, ch) for op in modes for ch in range(CHUNKS)]
        x_raw = {(op, j): sbuf("x_raw_%s%d" % (op, j), [P, K], BF16) for op in modes for j in range(E // P)}
        x_stage = {op: ring("x_stage_" + op, PASSES, [P, PACK * CHUNK], BF16) for op in modes}
        x_codes = {key: sbuf("x_codes_%s%d" % key, [P, PASSES * CHUNK], U32) for key in x_keys}
        x_scales = {key: sbuf("x_scales_%s%d" % key, [P, PASSES * CHUNK], U8) for key in x_keys}
        g_keys = [(g, c) for g in range(GROUPS) for c in range(PASSES)]
        g_raw = {key: sbuf("g_raw%d%d" % key, [P, PACK, GROUP], BF16) for key in g_keys}
        g_stage = [ring("g_stage%d" % c, 2, [P, PACK * 2 * P], BF16) for c in range(PASSES)]
        g_codes = {key: sbuf("g_codes%d%d" % key, [P, GROUP], U32) for key in g_keys}
        g_scales = {key: sbuf("g_scales%d%d" % key, [P, GROUP], U8) for key in g_keys}
        d_raw = ring("d_raw", len(STEPS), [P, TILES, GROUP], BF16)
        rc_rows = sbuf("rc_rows", [P, GROUP], BF16)
        rc_cols = sbuf("rc_cols", [P, 2 * GROUPS, PACK], F32)
        ident = sbuf("ident", [P, P], F32)
        work = ring("work", WORK_RING, [P, 2 * BANK], F32)
        y_slots = ring("y_slots", WORK_RING, [P, 2 * BANK], F32)
        y_packed = ring("y_packed", PACK_RING, [P, PACK * CHUNK], BF16)
        y_out = ring("y_out", OUT_RING, [P, GROUP], F32)
        y_codes = ring("y_codes", len(STEPS), [P, CHUNK], U32)
        y_scales = sbuf("y_scales", [P, E], U8)

        nc.vector.memset(rc_rows[:].bitcast(I32), 0)
        make_identity(nc, ident[:])

        def load_d(s):
            ch, g = STEPS[s]
            rows = stiffness[ch * CHUNK : (ch + 1) * CHUNK, g * GROUP : (g + 1) * GROUP]
            nc.sync.dma_start(out=d_raw[s][:], in_=rows.rearrange("(j p) n -> p j n", p=P))

        first_ch = [min(s for s, step in enumerate(STEPS) if step[0] == ch) for ch in range(CHUNKS)]
        first_g = [min(s for s, step in enumerate(STEPS) if step[1] == g) for g in range(GROUPS)]
        for s, (ch, g) in enumerate(STEPS):
            for c, op in enumerate(modes):
                if first_ch[ch] == s:
                    for j in range(ch * TILES, (ch + 1) * TILES):
                        nc.sync.dma_start(out=x_raw[op, j][:], in_=modes[op][j * P : (j + 1) * P, :])
                if first_g[g] == s:
                    rows = gradient[c * GROUP : (c + 1) * GROUP, g * GROUP : (g + 1) * GROUP]
                    nc.sync.dma_start(out=g_raw[g, c][:], in_=rows.rearrange("(p j) n -> p j n", j=PACK))
            if s == 0:
                for i, vec in enumerate((relaxation, prestress)):
                    rows = vec.rearrange("(g n) -> g n", n=GROUP)
                    nc.sync.dma_start(out=rc_rows[i * GROUPS : (i + 1) * GROUPS, :], in_=rows)
            else:
                load_d(s - 1)
        load_d(LAST)

        def quantize(codes, scales, src):
            nc.vector.quantize_mx(out=codes.bitcast(FP8X4), scales=scales, in_=src)

        def turn_pairs(bank, col0, width, rows):
            pairs = rows.bitcast(F32)
            for u in range(2):
                lo = u * width + col0
                nc.tensor.transpose(bank[:, lo : lo + P], pairs[:, u::2], ident[:])

        staged = []

        def quantize_staged(keep=0):
            while len(staged) > keep:
                quantize(*staged.pop(0))

        def g_half(g, c, u, copy):
            dst = g_stage[c][u]
            src = g_raw[g, c][:].rearrange("p j (a b t) -> p a j b t", b=2, t=PACK)[:, :, :, :, 2 * u : 2 * u + 2]
            copy(out=dst[:].rearrange("p (t a b j) -> p a j b t", t=2, b=2, j=PACK), in_=src)
            cols = slice(2 * u * P, 2 * (u + 1) * P)
            staged.append((g_codes[g, c][:, cols], g_scales[g, c][:, cols], dst[:]))

        def x_turn(op, c, ch, bank):
            for j in range(TILES):
                turn_pairs(bank, j * P, CHUNK, x_raw[op, ch * TILES + j][:, c * GROUP : (c + 1) * GROUP])

        def x_out(op, c, ch, bank):
            dst = x_stage[op][c]
            nc.scalar.copy(
                out=dst[:].bitcast(F32).rearrange("p (e u) -> p e u", u=2),
                in_=bank[:].rearrange("p (u e) -> p e u", u=2),
            )
            cols = slice(c * CHUNK, (c + 1) * CHUNK)
            staged.append((x_codes[op, ch][:, cols], x_scales[op, ch][:, cols], dst[:]))

        def runs(s, h):
            if s == LAST:
                return [(t, h * P, P) for t in range(PACK)]
            return [(t, 0, CHUNK) for t in (2 * h, 2 * h + 1)]

        def mx(out, g, t, op, ch, c, e0, w, start, stop):
            x_cols = slice(c * CHUNK + e0, c * CHUNK + e0 + w)
            nc.tensor.matmul_mx(
                out=out,
                lhsT=g_codes[g, c][:, t * P : (t + 1) * P].bitcast(FP8X4),
                lhsT_scale=g_scales[g, c][:, t * P : (t + 1) * P],
                rhs=x_codes[op, ch][:, x_cols].bitcast(FP8X4),
                rhs_scale=x_scales[op, ch][:, x_cols],
                start=start,
                stop=stop,
            )

        def multiply(s):
            ch, g = STEPS[s]
            order = [(op, pair, h) for op, pair in (("v", rate_banks), ("u", strain_banks)) for h in range(2)]
            if s in (0, LAST):
                order = sorted(order, key=lambda item: item[2])
            for op, pair, h in order:
                for i, (t, e0, w) in enumerate(runs(s, h)):
                    for c in range(PASSES):
                        mx(pair[h][:, i * w : (i + 1) * w], g, t, op, ch, c, e0, w, c == 0, c == PASSES - 1)

        def half(s, h):
            return work[s % WORK_RING][:, h * BANK : (h + 1) * BANK]

        def scale_rate(s, h):
            for i, (t, e0, w) in enumerate(runs(s, h)):
                cols = slice(i * w, (i + 1) * w)
                r_col = rc_cols[:, STEPS[s][1], t : t + 1]
                nc.scalar.activation(out=half(s, h)[:, cols], in_=rate_banks[h][:, cols], func=ACT.Copy, scale=r_col)

        def add_strain(s, h):
            nc.vector.tensor_tensor(out=half(s, h), in0=strain_banks[h][:], in1=half(s, h), op=ALU.add)

        def d_turn(s, bank):
            for j in range(TILES):
                turn_pairs(bank, j * P, CHUNK, d_raw[s][:, j, :])

        def times_d(s, h, bank):
            if s == LAST:
                d_t = bank[:].bitcast(BF16).rearrange("p (u j e i) -> p j u i e", u=2, j=TILES, i=2)[:, h, :, :, :]
                acc = half(s, h).rearrange("p (u i e) -> p u i e", u=2, i=2)
            else:
                d_t = bank[:, h * CHUNK : (h + 1) * CHUNK].bitcast(BF16).rearrange("p (e i) -> p i e", i=2)
                acc = half(s, h).rearrange("p (i e) -> p i e", i=2)
            nc.vector.tensor_tensor(out=acc, in0=d_t, in1=acc, op=ALU.mult)

        def add_c(s, h, i, engine):
            t, e0, w = runs(s, h)[i]
            cols = slice(h * BANK + i * w, h * BANK + (i + 1) * w)
            src, dst = work[s % WORK_RING][:, cols], y_slots[s % WORK_RING][:, cols]
            c_col = rc_cols[:, GROUPS + STEPS[s][1], t : t + 1]
            if engine is nc.scalar:
                nc.scalar.activation(out=dst, in_=src, func=ACT.Identity, bias=c_col)
            else:
                engine.tensor_scalar(out=dst, in0=src, scalar1=1.0, scalar2=c_col, op0=ALU.mult, op1=ALU.add)

        def y_turn(s, j, bank):
            for t in range(PACK):
                lo = (j * PACK + t) * P if s == LAST else t * CHUNK + j * P
                nc.tensor.transpose(bank[:, t * P : (t + 1) * P], y_slots[s % WORK_RING][:, lo : lo + P], ident[:])

        def y_store(s, j, bank):
            ch, g = STEPS[s]
            dst = y_out[(s * TILES + j) % OUT_RING]
            nc.scalar.copy(
                out=dst[:].rearrange("e (p t) -> e p t", t=PACK),
                in_=bank[:].rearrange("e (t p) -> e p t", t=PACK),
            )
            lo = ch * CHUNK + j * P
            nc.sync.dma_start(out=out_0[lo : lo + P, g * GROUP : (g + 1) * GROUP], in_=dst[:])

        packed = []

        def y_pack(s, e0, w):
            cols = slice(PACK * e0, PACK * (e0 + w))
            nc.vector.tensor_copy(
                out=y_packed[s % PACK_RING][:, cols].rearrange("p (a i t) -> p a t i", i=4, t=PACK),
                in_=y_slots[s % WORK_RING][:, cols].rearrange("p (t a i) -> p a t i", t=PACK, i=4),
            )
            packed.append((s, e0, w))

        def quantize_packed():
            while packed:
                s, e0, w = packed.pop(0)
                ch, g = STEPS[s]
                lo = ch * CHUNK
                src = y_packed[s % PACK_RING][:, PACK * e0 : PACK * (e0 + w)]
                quantize(y_codes[s][:, e0 : e0 + w], y_scales[4 * g :, lo + e0 : lo + e0 + w], src)
                if e0 + w == CHUNK:
                    words = out_1[g, :, lo : lo + CHUNK, :].rearrange("p m t -> p (m t)").bitcast(I32)
                    nc.sync.dma_start(out=words, in_=y_codes[s][:].bitcast(I32))

        turned = []

        def empty_turned(keep=0):
            while len(turned) > keep:
                bank, empty, item = turned.pop(0)
                empty(*item, bank)

        def free(bank):
            while any(bank is entry[0] for entry in turned):
                empty_turned(keep=len(turned) - 1)

        def turn(fill, empty, item, bank):
            free(bank)
            fill(*item, bank)
            turned.append((bank, empty, item))

        for i, op in enumerate(modes):
            for c in range(PASSES):
                x_turn(op, c, 0, banks[PASSES * i + c])
            x_out(op, 0, 0, banks[PASSES * i])
            quantize_staged(keep=1)
            g_half(0, i, 0, nc.vector.tensor_copy)
            x_out(op, 1, 0, banks[PASSES * i + 1])
            g_half(0, i, 1, nc.scalar.copy)
        quantize_staged(keep=1)
        for i in range(WARM_UP):
            mx(y_banks[0][:, 0:CHUNK], 0, 0, "v", 0, 0, 0, CHUNK, True, True)
        turn_pairs(d_bank, 0, P, rc_rows[:])
        rc_pairs = d_bank[:, 0 : 2 * P].bitcast(BF16).rearrange("p (u r i) -> p u r i", u=2, i=2)
        nc.vector.tensor_copy(out=rc_cols[:].rearrange("p r (u i) -> p u r i", u=2), in_=rc_pairs[:, :, 0 : 2 * GROUPS, :])
        quantize_staged()

        x_todo = [(op, c, ch) for ch in range(1, CHUNKS) for op in modes for c in range(PASSES)]
        g2_halves = [(2, c, u) for c in range(PASSES) for u in range(2)]
        g2_plan = {1 + i: item for i, item in enumerate(g2_halves)}
        y_todo = [(s, j) for s in range(LAST) for j in range(TILES)]
        pack_todo = list(range(LAST))

        for s in range(len(STEPS)):
            multiply(s)
            if s == 1:
                g_half(1, 1, 0, nc.vector.tensor_copy)
                quantize_staged()
            if s >= 1:
                for h in range(2):
                    times_d(s - 1, h, d_bank)
                    for i in range(2 - h if s < LAST else 0):
                        add_c(s - 1, h, i, nc.gpsimd)
            empty_turned(keep=1)
            scale_rate(s, 0)
            if s == LAST:
                break
            scale_rate(s, 1)
            empty_turned()
            if s == 1:
                g_half(1, 1, 1, nc.scalar.copy)
            if s in g2_plan and g2_plan[s][2] == 1:
                g_half(*g2_plan[s], nc.scalar.copy)
            if s >= 1:
                add_c(s - 1, 1, 1, nc.scalar)
            for h in range(2):
                add_strain(s, h)
            quantize_packed()
            quantize_staged()
            lag = LAG if s < CATCH_UP else 1
            while pack_todo and pack_todo[0] <= s - lag:
                y_pack(pack_todo.pop(0), 0, CHUNK)
            if s in g2_plan and g2_plan[s][2] == 0:
                g_half(*g2_plan[s], nc.vector.tensor_copy)
            if s == 0:
                g_half(1, 0, 0, nc.vector.tensor_copy)
                not_yet = staged.pop()
                for bank in [x_bank] + y_banks + [x_bank]:
                    turn(x_turn, x_out, x_todo.pop(0), bank)
                empty_turned()
                quantize_staged()
                staged.append(not_yet)
                g_half(1, 0, 1, nc.scalar.copy)
                d_turn(0, d_bank)
                continue
            x_banks = [x_bank] if s >= LAG else [x_bank] + y_banks
            y_room = y_banks if x_todo or s + 1 == LAST else y_banks + [x_bank]
            for bank in x_banks[: len(x_todo)]:
                turn(x_turn, x_out, x_todo.pop(0), bank)
            d_turn(s, d_bank)
            for bank in y_room:
                if y_todo[0][0] <= s - lag:
                    turn(y_turn, y_store, y_todo.pop(0), bank)
            if s + 1 == LAST:
                free(x_bank)
                d_turn(LAST, x_bank)

        quantize_packed()
        for h in range(2):
            for i in range(2):
                add_c(LAST - 1, h, i, nc.vector)
        empty_turned()
        scale_rate(LAST, 1)
        add_strain(LAST, 0)
        y_pack(LAST - 1, 0, CHUNK)
        times_d(LAST, 0, x_bank)
        for j in range(TILES):
            y_turn(LAST - 1, j, y_banks[j])
        y_store(LAST - 1, 0, y_banks[0])
        for i in range(PACK):
            add_c(LAST, 0, i, nc.scalar)
        add_strain(LAST, 1)
        quantize_packed()
        times_d(LAST, 1, x_bank)
        y_store(LAST - 1, 1, y_banks[1])
        y_pack(LAST, 0, P)
        for i in range(PACK):
            add_c(LAST, 1, i, nc.scalar if i < 2 else nc.vector)
        quantize_packed()
        for j in range(TILES):
            y_turn(LAST, j, rate_banks[j])
        y_store(LAST, 0, rate_banks[0])
        y_pack(LAST, P, P)
        quantize_packed()
        y_store(LAST, 1, rate_banks[1])
        for q in range(4):
            queue = nc.scalar if q % 2 else nc.sync
            queue.dma_start(
                out=out_2[:, 4 * q : 4 * q + 4, :].bitcast(I32),
                in_=y_scales[32 * q : 32 * q + 4 * GROUPS, :].bitcast(I32),
            )
